import numpy as np, ml_dtypes
CORES = [16,32,48,64,80]
N = 5
CB = 64
def setup_inputs(rng):
    return {"x": rng.standard_normal((N, 128, N * CB), dtype=np.float32).astype(ml_dtypes.bfloat16)}
def setup_inputs_big(rng):
    d = setup_inputs(rng)
    for k in ("x",): d[k] = (d[k].astype(np.float32) * 1024.0).astype(d[k].dtype)
    return d
def setup_inputs_small(rng):
    d = setup_inputs(rng)
    for k in ("x",): d[k] = (d[k].astype(np.float32) * (1 / 1024.0)).astype(d[k].dtype)
    return d
def setup_inputs_apart(rng):
    d = setup_inputs(rng)
    f = (10.0 ** rng.permutation(np.linspace(-1.5, 1.5, N))).astype(np.float32).reshape(N, 1, 1)
    for k in ("x",): d[k] = (d[k].astype(np.float32) * f).astype(d[k].dtype)
    return d
def reference(x):
    X = x.astype(np.float64)
    G = sum(X[j].T @ X[j] for j in range(N))
    y = np.full((N, CB, N * CB), np.nan)
    for r in range(N):
        y[r][:, :CB * r] = G[CB * r:CB * r + CB, :CB * r]
    return {"y": y.astype(ml_dtypes.bfloat16 if x.dtype != np.float64 else np.float64)}

from concourse.bass import DstId, RemoteDMATransfer
from concourse.mybir import AluOpType

N = 5
CB = 64
H = CB // 2
PAIRS = ((4, 3), (2, 1))

SCRATCH = {
    "xs": ("sbuf", [128, N * CB], "bfloat16"),
    "ps0": ("psum", [128, 512], "float32"),
    "ps1": ("psum", [128, 512], "float32"),
    "snd0": ("sbuf", [128, H * 7], "bfloat16"),
    "snd1": ("sbuf", [128, H * 3], "bfloat16"),
    "land": ("sbuf", [128, N, H * 4], "bfloat16"),
    "res": ("sbuf", [128, H * 4], "bfloat16"),
}
SEMAPHORES = ["xin", "mm0", "mm1", "cp0", "cp1", "arr0", "arr1", "arr2", "arr3", "arr4", "acc", "done", "stored",
              "sent"]


def _col0(r):
    for gi, (big, small) in enumerate(PAIRS):
        if r == big:
            return gi, 0
        if r == small:
            return gi, H * big
    return None


def _calls(s):
    out = []
    for gi in ((0, 1) if s < 2 else (1, 0)):
        big, small = PAIRS[gi]
        if s not in (big, small):
            out.append((gi, [(big, 0, H * big, 0), (small, H * small, H * big, H * (big - small))]))
        else:
            r = small if s == big else big
            out.append((gi, [(r, _col0(r)[1], H * r, 0)]))
    return out


def _engine_shares(topo, cores, s, items):
    m = -1
    for it in items:
        m &= topo.mask(cores[s], cores[it[0]])
    bits = [b for b in range(64) if (m >> b) & 1]
    k = len(bits) // len(items)
    return [sum(1 << b for b in bits[i * k:(i + 1) * k]) for i in range(len(items))], k


def rank_program(g, core, T, topo):
    me = T.rank_of(core)
    if me is None:
        return
    cores = T.cores
    calls = _calls(me)

    g.sync.dma_start(T.xs[:], T.x[:]).then_inc(T.sem.xin, 16)
    g.tensor.wait_ge(T.sem.xin, 16)
    for gi, items in calls:
        ps = T["ps%d" % gi]
        for r in PAIRS[gi]:
            c0, w = _col0(r)[1], H * r
            blk = T.xs[:, CB * r:CB * r + CB]
            g.tensor.matmul(ps[0:64, c0:c0 + w], blk, T.xs[:, 0:w], start=True, stop=True).then_inc(
                T.sem["mm%d" % gi], 1)
            g.tensor.matmul(ps[64:128, c0:c0 + w], blk, T.xs[:, w:2 * w], start=True, stop=True).then_inc(
                T.sem["mm%d" % gi], 1)
    for gi, items in calls:
        lo = min(it[1] for it in items)
        hi = max(it[1] + it[2] for it in items)
        g.vector.wait_ge(T.sem["mm%d" % gi], 4)
        g.vector.tensor_copy(T["snd%d" % gi][:, lo:hi], T["ps%d" % gi][:, lo:hi]).then_inc(T.sem["cp%d" % gi], 1)

    sent = 0
    for gi, items in calls:
        masks, k = _engine_shares(topo, cores, me, items)
        trs = []
        for (r, lo, w, off), m in zip(items, masks):
            rid, pid, _se = topo.addr(cores[r])
            trs.append(RemoteDMATransfer(dst_ids=[DstId(rid=rid, pnc=pid)], dma_engine_mask=m,
                                         remote_sem=T.sem["arr%d" % me], src=T["snd%d" % gi][:, lo:lo + w],
                                         dst=T.land[:, me, 0:w]))
            sent += k
        g.wait_ge(T.sem["cp%d" % gi], 1)
        g.remote_dma_fused(trs, local_sem=T.sem.sent)

    if me >= 1:
        gi, c0 = _col0(me)
        w = H * me
        own = T["ps%d" % gi][:, c0:c0 + w]
        inc = []
        for s in range(N):
            if s == me:
                continue
            for pos, (_gi, items) in enumerate(_calls(s)):
                for it in items:
                    if it[0] == me:
                        inc.append((pos, s, it[3], _engine_shares(topo, cores, s, items)[1]))
        inc.sort()
        for n, (pos, s, off, k) in enumerate(inc):
            g.vector.wait_ge(T.sem["arr%d" % s], k)
            if n:
                g.vector.wait_ge(T.sem.acc, n)
            last = n == len(inc) - 1
            g.vector.tensor_tensor(T.res[:, 0:w] if last else own, own, T.land[:, s, off:off + w],
                                   AluOpType.add).then_inc(T.sem.done if last else T.sem.acc, 1)
        g.sync.wait_ge(T.sem.done, 1)
        g.sync.dma_start(T.y[:, 0:w], T.res[0:64, 0:w]).then_inc(T.sem.stored, 16)
        g.scalar.wait_ge(T.sem.done, 1)
        g.scalar.dma_start(T.y[:, w:2 * w], T.res[64:128, 0:w]).then_inc(T.sem.stored, 16)
        g.wait_ge(T.sem.stored, 32)
    g.wait_ge(T.sem.sent, sent)
